import numpy as np
import ml_dtypes


def mxq(x, axis, fmt="e4m3"):
    dtype, down = {"e4m3": (ml_dtypes.float8_e4m3fn, 7), "e5m2": (ml_dtypes.float8_e5m2, 14)}[fmt]
    v = np.moveaxis(np.asarray(x, np.float32).astype(ml_dtypes.bfloat16).astype(np.float64), axis, -1)
    blocks = v.reshape(v.shape[:-1] + (-1, 32))
    amax = np.abs(blocks).max(-1, keepdims=True)
    byte = np.maximum(np.where(amax > 0, np.frexp(amax)[1] - 1 + 127, 0) - down, 1)
    scale = np.exp2(byte - 127.0)
    codes = (blocks / scale).astype(np.float32).astype(dtype).astype(np.float64)
    return np.moveaxis((codes * scale).reshape(v.shape), -1, axis)


WIDE = False


def mx_kscale(k):
    if not WIDE:
        return np.ones(k)
    levels = np.array([10, -10, 5, -5, 0])
    if k % 512:
        return np.exp2(np.random.permutation(np.resize(levels, k // 32))).repeat(32)
    a = np.empty((k // 512, 16))
    for p in range(k // 512):
        a[p, :8] = np.random.permutation(np.resize(levels, 8))
        for g in range(8):
            far = levels[np.abs(levels - a[p, g]) >= 10]
            a[p, g + 8] = far[np.random.randint(len(far))]
    return np.exp2(a.ravel()).repeat(32)


BF16 = ml_dtypes.bfloat16


def bf(x):
    return np.asarray(x, np.float32).astype(BF16)


def f64(x):
    return np.asarray(x).astype(np.float64)


E2M1 = np.array([0.0, 0.5, 1.0, 1.5, 2.0, 3.0, 4.0, 6.0, -0.0, -0.5, -1.0, -1.5, -2.0, -3.0, -4.0, -6.0])


def pack_weight(w, fmt):
    k, n = w.shape
    w = f64(bf(w)).reshape(k // 32, 32, n)
    amax = np.abs(w).max(1)
    if fmt == "e4m3":
        byte = np.frexp(amax)[1] - 1 + 127 - 7
    else:
        mant, ex = np.frexp(amax / 6.0)
        byte = np.where(mant > 0.5, ex, ex - 1) + 127
    byte = np.clip(np.where(amax > 0, byte, 1), 1, 254)
    scaled = (w * np.exp2(127.0 - byte)[:, None, :]).reshape(k, n).astype(np.float32)
    by_word = np.ascontiguousarray(scaled.reshape(k // 512, 128, 4, n).transpose(0, 1, 3, 2))
    if fmt == "e4m3":
        words = by_word.astype(ml_dtypes.float8_e4m3fn).view(np.uint8)
    else:
        c = by_word.astype(ml_dtypes.float4_e2m1fn).view(np.uint8) & 0xF
        words = c[..., 0::2] | (c[..., 1::2] << 4)
    return np.ascontiguousarray(words), np.ascontiguousarray(byte.astype(np.uint8).reshape(k // 512, 16, n))


def unpack_weight(words, scales, fmt):
    g, p, n, _ = words.shape
    if fmt == "e4m3":
        vals = np.ascontiguousarray(words).view(ml_dtypes.float8_e4m3fn).astype(np.float64)
    else:
        nib = np.empty((g, p, n, 4), np.uint8)
        nib[..., 0::2] = words & 0xF
        nib[..., 1::2] = words >> 4
        vals = E2M1[nib]
    vals = vals * np.repeat(np.exp2(scales.astype(np.float64) - 127.0), 8, axis=1)[..., None]
    return vals.transpose(0, 1, 3, 2).reshape(g * 512, n)
def pack4(w):
    words, scales = pack_weight(w, "e2m1")
    return words.reshape(words.shape[0], 128, -1), scales


def unpack4(words, scales):
    return unpack_weight(words.reshape(words.shape[0], 128, -1, 2), scales, "e2m1")


def planes(Y):
    n, m = Y.shape
    b = f64(bf(Y)).reshape(n // 32, 32, m)
    amax = np.abs(b).max(1)
    byte = np.clip(np.where(amax > 0, np.frexp(amax)[1] - 1 + 127 - 7, 1), 1, 254)
    codes = (b * np.exp2(127.0 - byte)[:, None, :]).reshape(n, m).astype(np.float32).astype(ml_dtypes.float8_e4m3fn).view(np.uint8)
    words = codes.reshape(n // 512, 128, 4, m).transpose(0, 1, 3, 2)
    return np.ascontiguousarray(words), np.ascontiguousarray(byte.astype(np.uint8).reshape(n // 512, 16, m))


S, T, D, W, V, R = 1024, 2048, 512, 1024, 512, 64

LEN2 = 2.0

def record(n, means):
    v = np.repeat(means, n // R, axis=0) + 0.6 * np.random.randn(n, D)
    return np.sqrt(LEN2) * v / np.sqrt(np.sum(v ** 2, axis=1, keepdims=True))

def contrasts(n, m):
    tau = n * np.random.uniform(0.25, 0.75, m)
    side = np.where(np.arange(n)[:, None] < tau, -1.0 / tau, 1.0 / (n - tau))
    return side * np.exp(0.5 * np.random.randn(n, m))

def setup_inputs():
    sd, st, ss = mx_kscale(D), mx_kscale(T), mx_kscale(S)
    means = np.random.randn(R, D)
    c_words, c_scales = pack4(0.27 * np.sqrt(T) * contrasts(T, W) / st[:, None])
    return {
        "z": bf(record(S, means) * sd),
        "x": bf(record(T, means) / sd),
        "a": bf(np.exp(-LEN2) * np.exp(0.3 * np.random.randn(T)) * st),
        "b": bf(0.4 * np.exp(0.5 * np.random.randn(S, T)) * st),
        "c_words": c_words, "c_scales": c_scales,
        "h": bf(np.exp(0.4 * np.random.randn(S)) * ss),
        "e0": bf(np.random.randn(S, W) * ss[:, None]),
        "c2": bf(contrasts(S, V) / ss[:, None]),
        "r": bf(3.0 * np.exp(0.8 * np.random.randn(W))),
    }

def reference(z, x, a, b, c_words, c_scales, h, e0, c2, r):
    dots = mxq(f64(z), 1) @ mxq(f64(x), 1).T
    g = f64(b) + f64(a) * np.exp(dots)
    gc = mxq(g, 1) @ unpack4(c_words, c_scales)
    e = f64(e0) + f64(h)[:, None] * gc
    y = (mxq(f64(c2), 0).T @ mxq(e, 0)) * f64(r)
    Y = y.T
    words, scales = planes(Y)
    return y, words, scales

from contextlib import ExitStack

import concourse.mybir as mybir
from concourse.masks import make_identity

S, T, D, W, V = 1024, 2048, 512, 1024, 512
FLOPS = 2 * (S * T * D + S * T * W + V * S * W)

F32 = mybir.dt.float32
BF16 = mybir.dt.bfloat16
U32 = mybir.dt.uint32
I32 = mybir.dt.int32
U8 = mybir.dt.uint8
FP8X4 = mybir.dt.float8_e4m3fn_x4
FP4X4 = mybir.dt.float4_e2m1fn_x4
ALU = mybir.AluOpType
ACT = mybir.ActivationFunctionType

P = 128
GROUP = 512
HALF = 256

SCALAR_BANKS = [0, 1, 2]
SUM_BANKS = [6, 7]
BASE_BANKS = [3, 4, 5]
SCALAR_SHARE = [128, 128, 128, 256]
WARM_FIRST, WARM_BETWEEN = 5, 2


def tile_rbf_contrast_scan_k1_kernel(tc, z, x, a, b, c_words, c_scales, h, e0, c2, r, out_0, out_1, out_2):
    nc = tc.nc
    with ExitStack() as ctx:
        keep = ctx.enter_context(tc.tile_pool(name="keep", bufs=1))
        stage = ctx.enter_context(tc.tile_pool(name="stage", bufs=1))
        psum = ctx.enter_context(tc.psum_pool(name="psum", bufs=1))
        ctx.enter_context(tc.manual_schedule())

        def kept(name, shape, dtype):
            return keep.tile(shape, dtype, name=name, align_bytes=64)

        def staged(tag, shape, dtype, bufs):
            return stage.tile(shape, dtype, name=tag, tag=tag, bufs=bufs, align_bytes=64)

        def bank(number):
            return psum.tile([P, GROUP], F32, name="bank%d" % number, tag="bank%d" % number)

        ident = kept("ident", [P, P], F32)
        e0_raw = [kept("e0_raw%d" % sg, [P, 4, W], BF16) for sg in range(2)]
        c2_raw = [kept("c2_raw%d" % sg, [P, 4, V], BF16) for sg in range(2)]
        c_code = kept("c_code", [P, 4, 2 * W], U8)
        c_scale = kept("c_scale", [P, 4, W], U8)
        a_col = kept("a_col", [P, 4, 4], BF16)
        h_col = kept("h_col", [P, 2, 4], BF16)
        r_raw = kept("r_raw", [P, 2, 4], BF16)
        r_col = kept("r_col", [P, 2, 4], F32)
        z_code, z_scale = kept("z_code", [P, S], U32), kept("z_scale", [P, S], U8)
        x_code, x_scale = kept("x_code", [P, T], U32), kept("x_scale", [P, T], U8)
        g_code, g_scale = kept("g_code", [P, 4, S], U32), kept("g_scale", [P, 4, S], U8)
        e_code, e_scale = kept("e_code", [P, 2, W], U32), kept("e_scale", [P, 2, W], U8)
        c2_code, c2_scale = kept("c2_code", [P, 2, V], U32), kept("c2_scale", [P, 2, V], U8)
        e_rows = [[kept("e_rows%d_%d" % (sg, wg), [P, 4, GROUP], BF16) for wg in range(2)] for sg in range(2)]
        y_code = [kept("y_code%d" % wg, [P, V], U32) for wg in range(2)]
        y_scale = kept("y_scale", [P, 2, V], U8)
        warm = kept("warm", [P, GROUP], BF16)
        warm_out = kept("warm_out", [P, 1], F32)

        raw = {}
        held = {}

        nc.vector.memset(warm[:], 0.0)
        make_identity(nc, ident[:])
        nc.vector.memset(c_scale[:].rearrange("p g n -> p (g n)").bitcast(I32), 0)

        def by_slot(rows):
            return rows.rearrange("(m t) d -> m t d", t=4)

        def per_partition(vector):
            return vector.rearrange("(g p t) -> p g t", p=P, t=4)

        def load_rows(name, source, group, pairs):
            rows = kept("%s_raw%d_%d" % (name, group, pairs[0]), [P, 2 * len(pairs), D], BF16)
            slots = slice(2 * pairs[0], 2 * pairs[-1] + 2)
            nc.sync.dma_start(out=rows[:], in_=by_slot(source[GROUP * group : GROUP * (group + 1), :])[:, slots, :])
            for i, pair in enumerate(pairs):
                raw[name, group, pair] = rows[:, 2 * i : 2 * i + 2, :]

        def load_b(step):
            sg, tg = divmod(step, 4)
            rows = staged("rows_4k", [P, 4, GROUP], BF16, 5)
            nc.sync.dma_start(out=rows[:], in_=by_slot(b[GROUP * sg : GROUP * (sg + 1), GROUP * tg : GROUP * (tg + 1)]))
            raw["b", step] = rows

        def load_c_words(first):
            nc.sync.dma_start(
                out=c_code[:, first : first + 2, :].bitcast(I32),
                in_=c_words[first : first + 2, :, :].rearrange("g p n -> p g n").bitcast(I32),
            )

        nc.scalar.activation(out=warm_out[:], in_=warm[:, 0:1], func=ACT.Exp)

        for pair in range(2):
            load_rows("z", z, 0, [pair])
            load_rows("x", x, 0, [pair])
        load_rows("x", x, 1, [0, 1])
        load_b(0)
        nc.sync.dma_start(out=a_col[:], in_=per_partition(a))
        load_rows("x", x, 2, [0, 1])
        load_b(1)
        load_rows("x", x, 3, [0, 1])
        load_b(2)
        load_rows("z", z, 1, [0, 1])
        load_b(3)
        for quad in range(4):
            nc.sync.dma_start(
                out=c_scale[32 * quad : 32 * quad + 4, :, :].bitcast(I32),
                in_=c_scales[:, 4 * quad : 4 * quad + 4, :].rearrange("g r n -> r g n").bitcast(I32),
            )
        load_c_words(0)
        load_b(4)
        load_c_words(2)
        nc.sync.dma_start(out=h_col[:], in_=per_partition(h))
        nc.sync.dma_start(out=e0_raw[0][:], in_=by_slot(e0[0:GROUP, :]))
        for sg in range(2):
            nc.sync.dma_start(out=c2_raw[sg][:], in_=by_slot(c2[GROUP * sg : GROUP * (sg + 1), :]))
        nc.sync.dma_start(out=r_raw[:], in_=per_partition(r))
        nc.sync.dma_start(out=e0_raw[1][:], in_=by_slot(e0[GROUP : 2 * GROUP, :]))

        warm_bank = bank(BASE_BANKS[2])

        def keep_warm(count):
            for i in range(count):
                nc.tensor.matmul(out=warm_bank[:], lhsT=warm[:, 0:P], rhs=warm[:], start=True, stop=True)

        keep_warm(WARM_FIRST)

        taken = []

        def scalar_bank(with_sum_banks):
            ring = SCALAR_BANKS + SUM_BANKS if with_sum_banks else SCALAR_BANKS
            unused = [number for number in ring if number not in taken]
            number = unused[0] if unused else max(ring, key=lambda n: taken[::-1].index(n))
            taken.append(number)
            return bank(number)

        def copy_on(engine, out, in_):
            if engine == "vector":
                nc.vector.tensor_copy(out=out, in_=in_)
            else:
                nc.scalar.copy(out=out, in_=in_)

        def spread(engine, grouped, rows):
            if engine == "gpsimd":
                nc.gpsimd.tensor_scalar(
                    out=grouped, in0=rows.rearrange("p t c -> p c t"), scalar1=1.0, scalar2=1.0, op0=ALU.mult, op1=ALU.mult
                )
            else:
                copy_on(engine, grouped.rearrange("p (c i) t -> p c t i", i=4), rows.rearrange("p t (c i) -> p c t i", i=4))

        def quantize(grouped, code, scale):
            nc.vector.quantize_mx(out=code.bitcast(FP8X4), scales=scale, in_=grouped.rearrange("p c t -> p (c t)"))

        def port_tile(step):
            return staged("port_b" if step in (1, 7) else "port_a", [P, GROUP, 4], BF16, 1)

        def prepare(name, group, pairs, code, scale, grouped):
            turned = {}
            for pair in pairs:
                turned[pair] = scalar_bank(True)
                words = raw[name, group, pair].bitcast(F32)
                for u in range(2):
                    for slot in range(2):
                        col = HALF * u + P * slot
                        nc.tensor.transpose(turned[pair][:, col : col + P], words[:, slot, u:HALF:2], ident[:])
            for pair in pairs:
                target = grouped[:, HALF * pair : HALF * (pair + 1), :].rearrange("p c t -> p (c t)").bitcast(F32)
                nc.scalar.copy(out=target.rearrange("p (c u) -> p c u", u=2), in_=turned[pair][:].rearrange("p (u c) -> p c u", u=2))
            lo, hi = HALF * pairs[0], HALF * (pairs[-1] + 1)
            cols = slice(GROUP * group + lo, GROUP * group + hi)
            quantize(grouped[:, lo:hi, :], code[:, cols], scale[:, cols])

        def dots(step, t):
            sg, tg = divmod(step, 4)
            acc = scalar_bank(step < 3)
            held["dots", step, t] = acc
            xs = slice(GROUP * tg + P * t, GROUP * tg + P * (t + 1))
            ss = slice(GROUP * sg, GROUP * (sg + 1))
            nc.tensor.matmul_mx(
                out=acc[:],
                lhsT=x_code[:, xs].bitcast(FP8X4), lhsT_scale=x_scale[:, xs],
                rhs=z_code[:, ss].bitcast(FP8X4), rhs_scale=z_scale[:, ss],
                start=True, stop=True,
            )

        def exp(step, t):
            rbf = staged("rbf", [P, GROUP], F32, 5)
            nc.scalar.activation(out=rbf[:], in_=held["dots", step, t][:], func=ACT.Exp)
            held["rbf", step, t] = rbf

        def products(step, ts):
            for t in ts:
                dots(step, t)
                exp(step, t)

        def turn_b(step):
            words = raw["b", step][:].bitcast(F32)
            for u in range(2):
                turned = bank(BASE_BANKS[(2 * step + u) % 3])
                held["b", step, u] = turned
                if u == 0 and step in (3, 4):
                    nc.tensor.matmul_mx(
                        out=turned[:],
                        lhsT=x_code[:, 0:P].bitcast(FP8X4), lhsT_scale=x_scale[:, 0:P],
                        rhs=z_code[:, 0:GROUP].bitcast(FP8X4), rhs_scale=z_scale[:, 0:GROUP],
                        start=True, stop=True,
                    )
                for slot in range(4):
                    nc.tensor.transpose(turned[:, P * slot : P * (slot + 1)], words[:, slot, u:HALF:2], ident[:])

        def tables(step, ts):
            for t in ts:
                if t == 0:
                    held["g_rows", step] = staged("g_rows", [P, 4, GROUP], BF16, 2)
                base = held["b", step, t // 2][:].bitcast(BF16).rearrange("p (c e) -> p e c", e=2)
                nc.vector.scalar_tensor_tensor(
                    out=held["g_rows", step][:, t, :],
                    in0=held["rbf", step, t][:], scalar=a_col[:, step % 4, t : t + 1], in1=base[:, t % 2, :],
                    op0=ALU.mult, op1=ALU.add,
                )

        def spread_g(step, engine, lo, hi):
            if ("g", step) not in held:
                held["g", step] = port_tile(step)
            spread(engine, held["g", step][:, lo:hi, :], held["g_rows", step][:, :, lo:hi])

        def quantize_g(step, lo, hi):
            sg, tg = divmod(step, 4)
            cols = slice(GROUP * sg + lo, GROUP * sg + hi)
            quantize(held["g", step][:, lo:hi, :], g_code[:, tg, cols], g_scale[:, tg, cols])

        def passes(sg, total, tgs):
            wg, t = divmod(total, 4)
            ss = slice(GROUP * sg + P * t, GROUP * sg + P * (t + 1))
            for tg in tgs:
                if tg == 0:
                    held["gc", sg, total] = bank(total if sg else SUM_BANKS[total % 2])
                nc.tensor.matmul_mx(
                    out=held["gc", sg, total][:],
                    lhsT=g_code[:, tg, ss].bitcast(FP8X4), lhsT_scale=g_scale[:, tg, ss],
                    rhs=c_code[:, tg, 2 * GROUP * wg : 2 * GROUP * (wg + 1)].bitcast(FP4X4),
                    rhs_scale=c_scale[:, tg, GROUP * wg : GROUP * (wg + 1)],
                    start=(tg == 0), stop=(tg == 3),
                )

        def carry(sg, total):
            wg, t = divmod(total, 4)
            nc.vector.scalar_tensor_tensor(
                out=e_rows[sg][wg][:, t, :].rearrange("p (j m) -> p j m", j=4),
                in0=held["gc", sg, total][:].rearrange("p (m j) -> p j m", j=4),
                scalar=h_col[:, sg, t : t + 1],
                in1=e0_raw[sg][:, t, GROUP * wg : GROUP * (wg + 1)].rearrange("p (m j) -> p j m", j=4),
                op0=ALU.mult, op1=ALU.add,
            )

        early = {("c2", sg): (c2_raw[sg][:], c2_code[:, sg, :], c2_scale[:, sg, :]) for sg in range(2)}
        for wg in range(2):
            ws = slice(GROUP * wg, GROUP * (wg + 1))
            early["e", wg] = (e_rows[0][wg][:], e_code[:, 0, ws], e_scale[:, 0, ws])

        def spread_early(name, index):
            held[name, index] = staged("grouped_512", [P, GROUP, 4], BF16, 3)
            spread("scalar", held[name, index][:], early[name, index][0])

        def quantize_early(name, index):
            quantize(held[name, index][:], early[name, index][1], early[name, index][2])

        def spread_e(wg, j, engine):
            held["e_last", wg, j] = staged("grouped_128", [P, P, 4], BF16, 4)
            spread(engine, held["e_last", wg, j][:], e_rows[1][wg][:, :, P * j : P * (j + 1)])

        def quantize_e(wg, j):
            ws = slice(GROUP * wg + P * j, GROUP * wg + P * (j + 1))
            quantize(held["e_last", wg, j][:], e_code[:, 1, ws], e_scale[:, 1, ws])

        def final(wg, j, sg):
            if sg == 0:
                held["d", wg, j] = bank(4 * wg + j)
            ws = slice(GROUP * wg + P * j, GROUP * wg + P * (j + 1))
            nc.tensor.matmul_mx(
                out=held["d", wg, j][:],
                lhsT=e_code[:, sg, ws].bitcast(FP8X4), lhsT_scale=e_scale[:, sg, ws],
                rhs=c2_code[:, sg, :].bitcast(FP8X4), rhs_scale=c2_scale[:, sg, :],
                start=(sg == 0), stop=(sg == 1),
            )

        def scale_y(wg, j, engine):
            if ("y_rows", wg) not in held:
                held["y_rows", wg] = staged("y_rows", [P, 4, V], F32, 2)
            target, factor = held["y_rows", wg][:, j, :], r_col[:, wg, j : j + 1]
            if engine == "scalar":
                nc.scalar.activation(out=target, in_=held["d", wg, j][:], func=ACT.Copy, scale=factor)
            else:
                nc.vector.tensor_scalar(out=target, in0=held["d", wg, j][:], scalar1=factor, scalar2=None, op0=ALU.mult)

        def spread_y(wg, vh):
            held["y", wg, vh] = staged("grouped_256", [P, HALF, 4], BF16, 3)
            spread("vector", held["y", wg, vh][:], held["y_rows", wg][:, :, HALF * vh : HALF * (vh + 1)])

        def quantize_y(wg, vh):
            cols = slice(HALF * vh, HALF * (vh + 1))
            quantize(held["y", wg, vh][:], y_code[wg][:, cols], y_scale[:, wg, cols])

        def turn_y(wg, j, vt):
            if ("turned_y", wg, vt) not in held:
                held["turned_y", wg, vt] = bank(vt)
            nc.tensor.transpose(
                held["turned_y", wg, vt][:, P * j : P * (j + 1)], held["y_rows", wg][:, j, P * vt : P * (vt + 1)], ident[:]
            )

        def store_y(wg, vt, engine):
            tiles = 2 - wg
            if vt % tiles == 0:
                held["y_out"] = staged("rows_4k", [P, tiles, GROUP], F32, 5)
            copy_on(
                engine,
                held["y_out"][:, vt % tiles, :].rearrange("p (m j) -> p m j", j=4),
                held["turned_y", wg, vt][:].rearrange("p (j m) -> p m j", j=4),
            )
            if vt % tiles == tiles - 1:
                rows = out_0[P * (vt + 1 - tiles) : P * (vt + 1), GROUP * wg : GROUP * (wg + 1)]
                nc.sync.dma_start(out=rows.rearrange("(i p) w -> p i w", p=P), in_=held["y_out"][:])

        def store_codes(wg):
            nc.sync.dma_start(out=out_1[wg].rearrange("p m t -> p (m t)").bitcast(I32), in_=y_code[wg][:].bitcast(I32))

        first_z = staged("grouped_512", [P, GROUP, 4], BF16, 3)
        prepare("z", 0, [0], z_code, z_scale, first_z)
        first_x = staged("grouped_512", [P, GROUP, 4], BF16, 3)
        prepare("x", 0, [0], x_code, x_scale, first_x)
        keep_warm(WARM_BETWEEN)
        prepare("z", 0, [1], z_code, z_scale, first_z)
        prepare("x", 0, [1], x_code, x_scale, first_x)
        keep_warm(WARM_BETWEEN)
        second_x = staged("grouped_512", [P, GROUP, 4], BF16, 3)
        prepare("x", 1, [0, 1], x_code, x_scale, second_x)

        ahead = [("x", 2, x_code, x_scale), ("x", 3, x_code, x_scale), ("z", 1, z_code, z_scale)]
        for step in range(4):
            products(step, [0, 1])
            turn_b(step)
            products(step, [2, 3])
            if step > 0:
                spread_g(step - 1, "scalar", 0, SCALAR_SHARE[step - 1])
            tables(step, range(4))
            if step > 0:
                quantize_g(step - 1, 0, GROUP)
            if step < 3:
                name, group, code, scale = ahead[step]
                prepare(name, group, [0, 1], code, scale, port_tile(step))
                load_b(5 + step)
            spread_g(step, "gpsimd", SCALAR_SHARE[step], GROUP)
        passes(0, 0, [0])
        passes(0, 1, [0])

        products(4, [0, 1])
        turn_b(4)
        products(4, [2])
        spread_g(3, "scalar", 0, SCALAR_SHARE[3])
        products(4, [3])
        passes(0, 0, [1, 2])
        passes(0, 1, [1, 2])
        tables(4, [0, 1])
        quantize_g(3, 0, HALF)
        products(5, [0, 1, 2])
        passes(0, 0, [3])
        passes(0, 1, [3])
        tables(4, [2, 3])
        quantize_g(3, HALF, GROUP)
        spread_g(4, "gpsimd", 0, GROUP)

        products(5, [3])
        dots(6, 0)
        turn_b(5)
        carry(0, 0)
        carry(0, 1)
        exp(6, 0)
        dots(6, 1)
        passes(0, 2, range(4))
        spread_early("c2", 0)
        exp(6, 1)
        products(6, [2, 3])
        passes(0, 3, range(4))
        tables(5, range(4))
        quantize_g(4, 0, GROUP)
        spread_g(5, "gpsimd", 0, GROUP)
        nc.vector.tensor_copy(out=r_col[:], in_=r_raw[:])

        turn_b(6)
        carry(0, 2)
        carry(0, 3)
        spread_early("c2", 1)
        passes(0, 4, range(4))
        products(7, [0, 1])
        passes(0, 5, range(4))
        tables(6, range(4))
        quantize_early("c2", 0)
        quantize_g(5, 0, GROUP)
        spread_g(6, "gpsimd", 0, GROUP)
        carry(0, 4)

        turn_b(7)
        products(7, [2, 3])
        spread_early("e", 0)
        passes(0, 6, range(4))
        tables(7, [0])
        carry(0, 5)
        tables(7, [1, 2, 3])
        quantize_g(6, 0, GROUP)
        spread_g(7, "vector", 0, HALF)
        spread_g(7, "scalar", HALF, GROUP)

        passes(1, 0, [0, 1])
        passes(1, 1, [0, 1])
        passes(0, 7, range(4))
        passes(1, 2, [0, 1])
        passes(1, 3, [0, 1])
        for total in range(4):
            passes(1, total, [2])
        carry(0, 6)
        quantize_g(7, 0, HALF)
        quantize_g(7, HALF, GROUP)
        carry(0, 7)
        spread_early("e", 1)
        quantize_early("e", 0)
        for total in range(4):
            passes(1, total, [3])
        for total in range(4):
            carry(1, total)

        passes(1, 4, range(4))
        passes(1, 5, range(4))
        for j in range(4):
            final(0, j, 0)
        passes(1, 6, range(3))
        quantize_early("c2", 1)
        for j in range(4):
            spread_e(0, j, "scalar" if j < 2 else "vector")
        for j in (2, 0, 1, 3):
            quantize_e(0, j)
            final(0, j, 1)
            scale_y(0, j, "scalar")
        passes(1, 6, [3])
        passes(1, 7, range(4))
        carry(1, 4)
        carry(1, 5)
        quantize_early("e", 1)
        carry(1, 6)
        carry(1, 7)
        for vt in range(4):
            for j in range(4):
                turn_y(0, j, vt)

        for j in range(4):
            final(1, j, 0)
        spread_y(0, 0)
        for j in range(4):
            spread_e(1, j, "scalar" if j == 0 else "vector")
        for vt in range(3):
            store_y(0, vt, "scalar")
        for j in range(4):
            quantize_e(1, j)
            final(1, j, 1)
        store_y(0, 3, "vector")
        scale_y(1, 0, "scalar")
        scale_y(1, 2, "vector")
        spread_y(0, 1)
        for vh in range(2):
            quantize_y(0, vh)
        store_codes(0)
        scale_y(1, 1, "scalar")
        scale_y(1, 3, "scalar")
        for j in (0, 2, 1, 3):
            for vt in range(4):
                turn_y(1, j, vt)
        for vh in range(2):
            spread_y(1, vh)
        for vt in range(3):
            store_y(1, vt, "scalar")
        for vh in range(2):
            quantize_y(1, vh)
        store_y(1, 3, "scalar")
        for quad in range(4):
            nc.sync.dma_start(
                out=out_2[:, 4 * quad : 4 * quad + 4, :].rearrange("n r m -> r n m").bitcast(I32),
                in_=y_scale[32 * quad : 32 * quad + 4, :, :].bitcast(I32),
            )
        store_codes(1)
